import numpy as np, ml_dtypes
CORES = [5,21,45,77,85,101,109,125,133,141,189,213]
N = 12
import mx_ref
NC, HD, G = 512, 1, 4
C, DEC = np.float32(0.023), np.float32(0.9)
BF = ml_dtypes.bfloat16
def cut(t, i, w=512):
    return t[:, w * i:w * i + w]
def tile(rs):
    return np.stack(rs, axis=2).reshape(128, -1).astype(BF)
def layer(w, X):
    out = []
    for i in range(G):
        for t in range(len(X)):
            p = mx_ref.matmul(mx_ref.quantize(cut(w, len(X) * i + t)), X[t])
            z = p if t == 0 else z + p
        out.append(z)
    return out
def pick(b):
    s = np.zeros((128, 128, 4), np.float32)
    s[np.arange(128), np.arange(128), b] = 1.0
    return mx_ref.quantize(s.reshape(128, 512).astype(BF))
def setup_inputs(rng):
    def f(*shape):
        return mx_ref.flush((rng.standard_normal(shape, dtype=np.float32) * np.exp2(rng.integers(-2, 3, shape[:-1] + (1,)))).astype(BF))
    return {"k": f(N, 128, HD * 4 * 512), "v": f(N, 128, HD * 512), "q": f(N, 128, HD * 4 * NC)}
def setup_inputs_blocks(rng):
    d = setup_inputs(rng)
    for k in ("k", "v", "q"): d[k] = mx_ref.spread(d[k], rng, 4)
    return d
def setup_inputs_wide(rng):
    d = setup_inputs(rng)
    for k in ("k", "v", "q"): d[k] = mx_ref.flush((d[k].astype(np.float32) * np.exp2(rng.integers(-4, 5, (N, 1, 1))).astype(np.float32)).astype(BF))
    return d
def setup_inputs_zeros(rng):
    d = setup_inputs(rng); v = d["v"].reshape(N, 128, -1, 4).copy()
    v[np.broadcast_to((rng.random((N, 1, v.shape[2], 1)) < 0.33), v.shape)] = 0
    d["v"] = v.reshape(d["v"].shape)
    return d
def reference(k, v, q):
    S = [pick(t) for t in range(4)]
    y = np.zeros((N, 128, HD * NC), np.float32)
    for a in range(HD):
        for r in range(N):
            R = [z * C for z in layer(cut(k[r], a, 4 * 512), [mx_ref.quantize(cut(v[r], a))])]
            if r > 0: R = [R[t] + mx_ref.matmul(S[t], s) * DEC for t in range(4)]
            s = mx_ref.quantize(tile(R))
            y[r][:, NC * a:NC * a + NC] = mx_ref.matmul(s, mx_ref.quantize(cut(q[r], a, 4 * NC)))
    return {"y": y}

@@ -1,0 +1,163 @@
+from concourse.mybir import dt, AluOpType, ActivationFunctionType
+
+SIM_CORES = 256
+W = 128
+SCRATCH = {
+    "vt": ("sbuf", [128, 512], "bfloat16"), "vc": ("sbuf", [128, 128], "float8_e4m3fn_x4"), "vs": ("sbuf", [128, 128], "uint8"),
+    "kt": ("sbuf", [128, 2048], "bfloat16"), "kc": ("sbuf", [128, 512], "float8_e4m3fn_x4"), "ks": ("sbuf", [128, 512], "uint8"),
+    "qt": ("sbuf", [128, 2048], "bfloat16"), "qc": ("sbuf", [128, 512], "float8_e4m3fn_x4"), "qs": ("sbuf", [128, 512], "uint8"),
+    "w": ("sbuf", [128, 520], "bfloat16"), "pc": ("sbuf", [128, 512], "float8_e4m3fn_x4"), "ps": ("sbuf", [128, 512], "uint8"),
+    "zc": ("sbuf", [128, 512], "float32"), "dm": ("sbuf", [128, 512], "float32"), "tile": ("sbuf", [128, 512], "bfloat16"),
+    "sc": ("sbuf", [128, 128], "float8_e4m3fn_x4"), "ss": ("sbuf", [128, 128], "uint8"),
+    "ac": ("sbuf", [128, 128], "float8_e4m3fn_x4"), "as": ("sbuf", [128, 128], "uint8"),
+    "yo": ("sbuf", [128, 512], "float32"),
+    "pz": ("psum", [128, 2048], "float32"), "pd": ("psum", [128, 2048], "float32"),
+}
+SEMAPHORES = (["lv", "lq", "one", "sel", "qv", "qp", "qq", "add", "qst", "arr", "sent", "sta", "stb"]
+              + [n + str(b) for n in ("lk", "qk", "z", "c", "d", "m", "y", "e") for b in range(4)])
+
+
+def engines(mask, n):
+    bits = [b for b in range(16) if mask >> b & 1][:n]
+    return sum(1 << b for b in bits), len(bits)
+
+
+def plan(T, topo):
+    hops = []
+    for src, dst in zip(T.cores[:-1], T.cores[1:]):
+        if topo.may_write(src, dst):
+            hops.append((src, dst, None, None))
+            continue
+        own = [c for c in range(SIM_CORES) if topo.host(c) == topo.host(src) and topo.chip(c) == topo.chip(src)
+               and topo.may_write(c, dst)]
+        near = [c for c in own if topo.die(c) == topo.die(src)]
+        far = [c for c in own if topo.die(c) != topo.die(src)]
+        hops.append((src, dst, near[0], far[0]))
+    return hops
+
+
+def send(g, T, topo, core, dst, out, in_, n):
+    mask, n = engines(topo.mask(core, dst), n)
+    rid, pid = topo.addr(dst, core)
+    g.remote_dma(out, in_, T.sem.arr, T.sem.sent, pid, rid, mask)
+    return n
+
+
+NE_CODES, NE_SCALES = 8, 8
+
+
+def rank_program(g, core, T, topo):
+    sem, cast = T.sem, dt.uint8
+    hops = plan(T, topo)
+    rank = T.rank_of(core)
+    if rank is None:
+        for src, dst, rc, rs in hops:
+            if core == rc:
+                g.wait_ge(sem.arr, NE_CODES)
+                n = send(g, T, topo, core, dst, T["ac"][:].bitcast(cast), T["ac"][:].bitcast(cast), NE_CODES)
+                g.wait_ge(sem.sent, n)
+            elif core == rs:
+                g.wait_ge(sem.arr, NE_SCALES)
+                n = send(g, T, topo, core, dst, T["as"][:], T["as"][:], NE_SCALES)
+                g.wait_ge(sem.sent, n)
+        return
+
+    te, ve, sc, sy = g.tensor, g.vector, g.scalar, g.sync
+    copy = ActivationFunctionType.Copy
+
+    def w(a, b=W):
+        return slice(a * b, a * b + b)
+
+    def bank(buf, b):
+        return buf[:, 512 * b:512 * b + W]
+
+    sy.dma_start(T.vt[:], T.v[:]).then_inc(sem.lv, 16)
+    for b in range(4):
+        (sc if b % 2 == 0 else sy).dma_start(T.kt[:, w(b, 512)], T.k[:, w(b, 512)]).then_inc(sem["lk%d" % b], 16)
+    if rank == 0:
+        for b in range(4):
+            sy.wait_ge(sem["lk%d" % b], 16)
+    sy.dma_start(T.qt[:], T.q[:]).then_inc(sem.lq, 16)
+
+    if rank > 0:
+        ve.memset(T.w[:], 1.0).then_inc(sem.one, 1)
+        g.wait_ge(sem.one, 1)
+        g.affine_select(T.w[:], T.w[:], [[-1, 520]], AluOpType.is_equal, 0.0, 3, 4).then_inc(sem.sel, 1)
+    ve.wait_ge(sem.lv, 16)
+    ve.quantize_mx(T.vc[:], T.vs[:], T.vt[:]).then_inc(sem.qv, 1)
+    for b in range(4):
+        ve.wait_ge(sem["lk%d" % b], 16)
+        ve.quantize_mx(T.kc[:, w(b)], T.ks[:, w(b)], T.kt[:, w(b, 512)]).then_inc(sem["qk%d" % b], 1)
+    if rank > 0:
+        ve.wait_ge(sem.sel, 1)
+        for b in range(4):
+            ve.quantize_mx(T.pc[:, w(b)], T.ps[:, w(b)], T.w[:, 3 - b:3 - b + 512]).then_inc(sem.qp, 1)
+        ve.wait_ge(sem.lq, 16)
+        ve.quantize_mx(T.qc[:], T.qs[:], T.qt[:]).then_inc(sem.qq, 1)
+
+    te.wait_ge(sem.qv, 1)
+    for b in range(4):
+        te.wait_ge(sem["qk%d" % b], 1)
+        te.matmul_mx(bank(T.pz, b), T.kc[:, w(b)], T.ks[:, w(b)], T.vc[:], T.vs[:], True, True).then_inc(sem["z%d" % b], 1)
+
+    if rank == 0:
+        for b in range(4):
+            eng = ve if b == 3 else sc
+            eng.wait_ge(sem["z%d" % b], 1)
+            out = T.tile[:, b:512:4]
+            if b == 3:
+                ve.tensor_scalar(out, bank(T.pz, b), 0.023, None, AluOpType.mult).then_inc(sem["c%d" % b], 1)
+            else:
+                sc.activation(out, bank(T.pz, b), copy, scale=0.023).then_inc(sem["c%d" % b], 1)
+        for b in range(4):
+            ve.wait_ge(sem["c%d" % b], 1)
+    else:
+        for b in range(4):
+            sc.wait_ge(sem["z%d" % b], 1)
+            sc.activation(T.zc[:, w(b)], bank(T.pz, b), copy, scale=0.023).then_inc(sem["c%d" % b], 1)
+        te.wait_ge(sem.qp, 4)
+        te.wait_ge(sem.arr, NE_CODES + NE_SCALES)
+        for b in range(4):
+            te.matmul_mx(bank(T.pd, b), T.pc[:, w(b)], T.ps[:, w(b)], T["ac"][:], T["as"][:], True, True).then_inc(sem["d%d" % b], 1)
+        for b in range(4):
+            sc.wait_ge(sem["d%d" % b], 1)
+            sc.activation(T.dm[:, w(b)], bank(T.pd, b), copy, scale=0.9).then_inc(sem["m%d" % b], 1)
+        for b in range(4):
+            ve.wait_ge(sem["c%d" % b], 1)
+        for b in range(4):
+            ve.wait_ge(sem["m%d" % b], 1)
+            ve.tensor_tensor(T.tile[:, b:512:4], T.zc[:, w(b)], T.dm[:, w(b)], AluOpType.add).then_inc(sem.add, 1)
+        ve.wait_ge(sem.add, 4)
+    ve.quantize_mx(T.sc[:], T.ss[:], T.tile[:]).then_inc(sem.qst, 1)
+
+    if rank < len(hops):
+        src, dst, rc, rs = hops[rank]
+        g.wait_ge(sem.qst, 1)
+        n = send(g, T, topo, core, dst if rc is None else rc, T["ac"][:].bitcast(cast), T.sc[:].bitcast(cast), NE_CODES)
+        n += send(g, T, topo, core, dst if rs is None else rs, T["as"][:], T.ss[:], NE_SCALES)
+        g.wait_ge(sem.sent, n)
+
+    if rank == 0:
+        ve.wait_ge(sem.lq, 16)
+        ve.quantize_mx(T.qc[:], T.qs[:], T.qt[:]).then_inc(sem.qq, 1)
+    for b in range(4):
+        te.wait_ge(sem["c%d" % b], 1)
+    te.wait_ge(sem.qq, 1)
+    te.wait_ge(sem.qst, 1)
+    for b in range(4):
+        te.matmul_mx(bank(T.pz, b), T.sc[:], T.ss[:], T.qc[:, w(b)], T.qs[:, w(b)], True, True).then_inc(sem["y%d" % b], 1)
+    for b in range(4):
+        if b % 2 == 0:
+            sc.wait_ge(sem["y%d" % b], 1)
+            sc.activation(T.yo[:, w(b)], bank(T.pz, b), copy).then_inc(sem["e%d" % b], 1)
+        else:
+            ve.wait_ge(sem["y%d" % b], 1)
+            ve.tensor_copy(T.yo[:, w(b)], bank(T.pz, b)).then_inc(sem["e%d" % b], 1)
+    sy.wait_ge(sem.e0, 1)
+    sy.wait_ge(sem.e1, 1)
+    sy.dma_start(T.y[:, w(0, 256)], T.yo[:, w(0, 256)]).then_inc(sem.sta, 16)
+    sc.wait_ge(sem.e2, 1)
+    sc.wait_ge(sem.e3, 1)
+    sc.dma_start(T.y[:, w(1, 256)], T.yo[:, w(1, 256)]).then_inc(sem.stb, 16)
+    sy.wait_ge(sem.sta, 16)
+    sc.wait_ge(sem.stb, 16)

@@ -2,74 +2,79 @@ from concourse.mybir import dt, AluOpType, ActivationFunctionType
 
 SIM_CORES = 256
 W = 128
+CA = 32
+NE = 8
 SCRATCH = {
     "vt": ("sbuf", [128, 512], "bfloat16"), "vc": ("sbuf", [128, 128], "float8_e4m3fn_x4"), "vs": ("sbuf", [128, 128], "uint8"),
     "kt": ("sbuf", [128, 2048], "bfloat16"), "kc": ("sbuf", [128, 512], "float8_e4m3fn_x4"), "ks": ("sbuf", [128, 512], "uint8"),
     "qt": ("sbuf", [128, 2048], "bfloat16"), "qc": ("sbuf", [128, 512], "float8_e4m3fn_x4"), "qs": ("sbuf", [128, 512], "uint8"),
     "w": ("sbuf", [128, 520], "bfloat16"), "pc": ("sbuf", [128, 512], "float8_e4m3fn_x4"), "ps": ("sbuf", [128, 512], "uint8"),
-    "zc": ("sbuf", [128, 512], "float32"), "dm": ("sbuf", [128, 512], "float32"), "tile": ("sbuf", [128, 512], "bfloat16"),
-    "sc": ("sbuf", [128, 128], "float8_e4m3fn_x4"), "ss": ("sbuf", [128, 128], "uint8"),
+    "zc": ("sbuf", [128, 512], "float32"), "dm": ("sbuf", [128, 512], "float32"),
+    "ta": ("sbuf", [128, 512], "bfloat16"), "tb": ("sbuf", [128, 512], "bfloat16"),
+    "sc": ("sbuf", [128, W + CA], "float8_e4m3fn_x4"), "ss": ("sbuf", [128, W + CA], "uint8"),
     "ac": ("sbuf", [128, 128], "float8_e4m3fn_x4"), "as": ("sbuf", [128, 128], "uint8"),
+    "rc": ("sbuf", [128, 128], "float8_e4m3fn_x4"), "rs": ("sbuf", [128, 128], "uint8"),
     "yo": ("sbuf", [128, 512], "float32"),
     "pz": ("psum", [128, 2048], "float32"), "pd": ("psum", [128, 2048], "float32"),
 }
-SEMAPHORES = (["lv", "lq", "one", "sel", "qv", "qp", "qq", "add", "qst", "arr", "sent", "sta", "stb"]
-              + [n + str(b) for n in ("lk", "qk", "z", "c", "d", "m", "y", "e") for b in range(4)])
-
-
-def engines(mask, n):
-    bits = [b for b in range(16) if mask >> b & 1][:n]
-    return sum(1 << b for b in bits), len(bits)
+SEMAPHORES = (["lv", "lq", "one", "sel", "zero", "qv", "qp", "qq", "adda", "addb", "qa", "qst", "arr", "sent", "sta", "stb"]
+              + ["in%d" % i for i in range(3)]
+              + [n + str(b) for n in ("lk", "qk", "z", "c", "d", "m", "n", "y", "e") for b in range(4)])
 
 
 def plan(T, topo):
     hops = []
     for src, dst in zip(T.cores[:-1], T.cores[1:]):
-        if topo.may_write(src, dst):
-            hops.append((src, dst, None, None))
-            continue
-        own = [c for c in range(SIM_CORES) if topo.host(c) == topo.host(src) and topo.chip(c) == topo.chip(src)
-               and topo.may_write(c, dst)]
-        near = [c for c in own if topo.die(c) == topo.die(src)]
-        far = [c for c in own if topo.die(c) != topo.die(src)]
-        hops.append((src, dst, near[0], far[0]))
+        near = far = None
+        e0 = 0
+        if not topo.may_write(src, dst):
+            own = [c for c in range(SIM_CORES) if topo.host(c) == topo.host(src) and topo.chip(c) == topo.chip(src)
+                   and topo.may_write(c, dst)]
+            near = [c for c in own if topo.die(c) == topo.die(src)][0]
+            far = [c for c in own if topo.die(c) != topo.die(src)][0]
+            e0 = NE
+        hops.append((src, dst, [(True, "c", 0, CA, near, 0), (False, "c", CA, W, near, 0), (False, "s", 0, W, far, e0)]))
     return hops
 
 
-def send(g, T, topo, core, dst, out, in_, n):
-    mask, n = engines(topo.mask(core, dst), n)
-    rid, pid = topo.addr(dst, core)
-    g.remote_dma(out, in_, T.sem.arr, T.sem.sent, pid, rid, mask)
-    return n
+def send(g, T, topo, core, to, out, in_, rsem, e0=0):
+    bits = [b for b in range(16) if topo.mask(core, to) >> b & 1][e0:e0 + NE]
+    rid, pid = topo.addr(to, core)
+    g.remote_dma(out, in_, rsem, T.sem.sent, pid, rid, sum(1 << b for b in bits))
 
 
-NE_CODES, NE_SCALES = 8, 8
+def view(T, kind, buf, lo, hi):
+    return T[buf + "c"][:, lo:hi].bitcast(dt.uint8) if kind == "c" else T[buf + "s"][:, lo:hi]
 
 
 def rank_program(g, core, T, topo):
-    sem, cast = T.sem, dt.uint8
+    sem = T.sem
     hops = plan(T, topo)
     rank = T.rank_of(core)
     if rank is None:
-        for src, dst, rc, rs in hops:
-            if core == rc:
-                g.wait_ge(sem.arr, NE_CODES)
-                n = send(g, T, topo, core, dst, T["ac"][:].bitcast(cast), T["ac"][:].bitcast(cast), NE_CODES)
-                g.wait_ge(sem.sent, n)
-            elif core == rs:
-                g.wait_ge(sem.arr, NE_SCALES)
-                n = send(g, T, topo, core, dst, T["as"][:], T["as"][:], NE_SCALES)
-                g.wait_ge(sem.sent, n)
+        sent = 0
+        for src, dst, pieces in hops:
+            for i, (_, kind, lo, hi, via, _) in enumerate(pieces):
+                if via == core:
+                    g.wait_ge(sem["in%d" % i], NE)
+                    send(g, T, topo, core, dst, view(T, kind, "a", lo, hi), view(T, kind, "r", lo, hi), sem.arr)
+                    sent += NE
+        if sent:
+            g.wait_ge(sem.sent, sent)
         return
 
     te, ve, sc, sy = g.tensor, g.vector, g.scalar, g.sync
     copy = ActivationFunctionType.Copy
+    last = rank == len(hops)
 
     def w(a, b=W):
         return slice(a * b, a * b + b)
 
-    def bank(buf, b):
-        return buf[:, 512 * b:512 * b + W]
+    def part(a, lo, hi):
+        return slice(a * W + lo, a * W + hi)
+
+    def bank(buf, b, lo=0, hi=W):
+        return buf[:, 512 * b + lo:512 * b + hi]
 
     sy.dma_start(T.vt[:], T.v[:]).then_inc(sem.lv, 16)
     for b in range(4):
@@ -83,6 +88,9 @@ def rank_program(g, core, T, topo):
         ve.memset(T.w[:], 1.0).then_inc(sem.one, 1)
         g.wait_ge(sem.one, 1)
         g.affine_select(T.w[:], T.w[:], [[-1, 520]], AluOpType.is_equal, 0.0, 3, 4).then_inc(sem.sel, 1)
+    if not last:
+        ve.memset(T.ta[:, 4 * CA:512], 0.0).then_inc(sem.zero, 1)
+        ve.memset(T.tb[:, 4 * (W - CA):512], 0.0).then_inc(sem.zero, 1)
     ve.wait_ge(sem.lv, 16)
     ve.quantize_mx(T.vc[:], T.vs[:], T.vt[:]).then_inc(sem.qv, 1)
     for b in range(4):
@@ -94,48 +102,90 @@ def rank_program(g, core, T, topo):
             ve.quantize_mx(T.pc[:, w(b)], T.ps[:, w(b)], T.w[:, 3 - b:3 - b + 512]).then_inc(sem.qp, 1)
         ve.wait_ge(sem.lq, 16)
         ve.quantize_mx(T.qc[:], T.qs[:], T.qt[:]).then_inc(sem.qq, 1)
+    if not last:
+        ve.wait_ge(sem.zero, 2)
 
     te.wait_ge(sem.qv, 1)
     for b in range(4):
         te.wait_ge(sem["qk%d" % b], 1)
         te.matmul_mx(bank(T.pz, b), T.kc[:, w(b)], T.ks[:, w(b)], T.vc[:], T.vs[:], True, True).then_inc(sem["z%d" % b], 1)
 
+    def strip(b):
+        return T.ta[:, b:4 * CA:4]
+
+    def others(b):
+        return T.tb[:, b:4 * (W - CA):4]
+
+    def quantise_strip():
+        ve.quantize_mx(T.sc[:, 0:W], T.ss[:, 0:W], T.ta[:]).then_inc(sem.qa, 1)
+
+    def quantise_others():
+        ve.wait_ge(sem.qa, 1)
+        ve.quantize_mx(T.sc[:, CA:CA + W], T.ss[:, CA:CA + W], T.tb[:]).then_inc(sem.qst, 1)
+
     if rank == 0:
-        for b in range(4):
-            eng = ve if b == 3 else sc
-            eng.wait_ge(sem["z%d" % b], 1)
-            out = T.tile[:, b:512:4]
-            if b == 3:
-                ve.tensor_scalar(out, bank(T.pz, b), 0.023, None, AluOpType.mult).then_inc(sem["c%d" % b], 1)
-            else:
-                sc.activation(out, bank(T.pz, b), copy, scale=0.023).then_inc(sem["c%d" % b], 1)
+        for b in range(3):
+            sc.wait_ge(sem["z%d" % b], 1)
+            sc.activation(strip(b), bank(T.pz, b, 0, CA), copy, scale=0.023).then_inc(sem.adda, 1)
+            sc.activation(others(b), bank(T.pz, b, CA, W), copy, scale=0.023).then_inc(sem["c%d" % b], 1)
+        ve.wait_ge(sem.z3, 1)
+        ve.tensor_scalar(strip(3), bank(T.pz, 3, 0, CA), 0.023, None, AluOpType.mult).then_inc(sem.adda, 1)
+        ve.tensor_scalar(others(3), bank(T.pz, 3, CA, W), 0.023, None, AluOpType.mult).then_inc(sem.c3, 1)
+        ve.wait_ge(sem.adda, 4)
+        quantise_strip()
         for b in range(4):
             ve.wait_ge(sem["c%d" % b], 1)
+        quantise_others()
     else:
         for b in range(4):
             sc.wait_ge(sem["z%d" % b], 1)
             sc.activation(T.zc[:, w(b)], bank(T.pz, b), copy, scale=0.023).then_inc(sem["c%d" % b], 1)
         te.wait_ge(sem.qp, 4)
-        te.wait_ge(sem.arr, NE_CODES + NE_SCALES)
+        te.wait_ge(sem.arr, NE * len(hops[rank - 1][2]))
         for b in range(4):
             te.matmul_mx(bank(T.pd, b), T.pc[:, w(b)], T.ps[:, w(b)], T["ac"][:], T["as"][:], True, True).then_inc(sem["d%d" % b], 1)
-        for b in range(4):
-            sc.wait_ge(sem["d%d" % b], 1)
-            sc.activation(T.dm[:, w(b)], bank(T.pd, b), copy, scale=0.9).then_inc(sem["m%d" % b], 1)
+
+        def scale(b, lo, hi, name):
+            sc.activation(T.dm[:, part(b, lo, hi)], bank(T.pd, b, lo, hi), copy, scale=0.9).then_inc(sem["%s%d" % (name, b)], 1)
+
         for b in range(4):
             ve.wait_ge(sem["c%d" % b], 1)
-        for b in range(4):
-            ve.wait_ge(sem["m%d" % b], 1)
-            ve.tensor_tensor(T.tile[:, b:512:4], T.zc[:, w(b)], T.dm[:, w(b)], AluOpType.add).then_inc(sem.add, 1)
-        ve.wait_ge(sem.add, 4)
-    ve.quantize_mx(T.sc[:], T.ss[:], T.tile[:]).then_inc(sem.qst, 1)
+        if last:
+            for b in range(4):
+                sc.wait_ge(sem["d%d" % b], 1)
+                scale(b, 0, W, "m")
+            for b in range(4):
+                ve.wait_ge(sem["m%d" % b], 1)
+                ve.tensor_tensor(T.ta[:, b:512:4], T.zc[:, w(b)], T.dm[:, w(b)], AluOpType.add).then_inc(sem.adda, 1)
+            ve.wait_ge(sem.adda, 4)
+            ve.quantize_mx(T.sc[:, 0:W], T.ss[:, 0:W], T.ta[:]).then_inc(sem.qst, 1)
+        else:
+            for b in range(4):
+                sc.wait_ge(sem["d%d" % b], 1)
+                scale(b, 0, W if b < 2 else CA, "m")
+            for b in (2, 3):
+                scale(b, CA, W, "n")
+            for b in range(4):
+                ve.wait_ge(sem["m%d" % b], 1)
+                ve.tensor_tensor(strip(b), T.zc[:, part(b, 0, CA)], T.dm[:, part(b, 0, CA)], AluOpType.add).then_inc(sem.adda, 1)
+            ve.wait_ge(sem.adda, 4)
+            quantise_strip()
+            for b in range(4):
+                if b >= 2:
+                    ve.wait_ge(sem["n%d" % b], 1)
+                ve.tensor_tensor(others(b), T.zc[:, part(b, CA, W)], T.dm[:, part(b, CA, W)], AluOpType.add).then_inc(sem.addb, 1)
+            ve.wait_ge(sem.addb, 4)
+            quantise_others()
 
-    if rank < len(hops):
-        src, dst, rc, rs = hops[rank]
-        g.wait_ge(sem.qst, 1)
-        n = send(g, T, topo, core, dst if rc is None else rc, T["ac"][:].bitcast(cast), T.sc[:].bitcast(cast), NE_CODES)
-        n += send(g, T, topo, core, dst if rs is None else rs, T["as"][:], T.ss[:], NE_SCALES)
-        g.wait_ge(sem.sent, n)
+    if not last:
+        _, dst, pieces = hops[rank]
+        for i, (ahead, kind, lo, hi, via, e0) in enumerate(pieces):
+            g.wait_ge(sem.qa if ahead else sem.qst, 1)
+            if via is None:
+                send(g, T, topo, core, dst, view(T, kind, "a", lo, hi), view(T, kind, "s", lo, hi), sem.arr)
+            else:
+                send(g, T, topo, core, via, view(T, kind, "r", lo, hi), view(T, kind, "s", lo, hi), sem["in%d" % i], e0)
+        g.wait_ge(sem.sent, NE * len(pieces))
 
     if rank == 0:
         ve.wait_ge(sem.lq, 16)
@@ -143,9 +193,11 @@ def rank_program(g, core, T, topo):
     for b in range(4):
         te.wait_ge(sem["c%d" % b], 1)
     te.wait_ge(sem.qq, 1)
+    if not last:
+        te.wait_ge(sem.qa, 1)
     te.wait_ge(sem.qst, 1)
     for b in range(4):
-        te.matmul_mx(bank(T.pz, b), T.sc[:], T.ss[:], T.qc[:, w(b)], T.qs[:, w(b)], True, True).then_inc(sem["y%d" % b], 1)
+        te.matmul_mx(bank(T.pz, b), T.sc[:, 0:W], T.ss[:, 0:W], T.qc[:, w(b)], T.qs[:, w(b)], True, True).then_inc(sem["y%d" % b], 1)
     for b in range(4):
         if b % 2 == 0:
             sc.wait_ge(sem["y%d" % b], 1)

from concourse.mybir import dt, AluOpType, ActivationFunctionType

SIM_CORES = 256
W = 128
CA = 32
NE = 8
SCRATCH = {
    "vt": ("sbuf", [128, 512], "bfloat16"), "vc": ("sbuf", [128, 128], "float8_e4m3fn_x4"), "vs": ("sbuf", [128, 128], "uint8"),
    "kt": ("sbuf", [128, 2048], "bfloat16"), "kc": ("sbuf", [128, 512], "float8_e4m3fn_x4"), "ks": ("sbuf", [128, 512], "uint8"),
    "qt": ("sbuf", [128, 2048], "bfloat16"), "qc": ("sbuf", [128, 512], "float8_e4m3fn_x4"), "qs": ("sbuf", [128, 512], "uint8"),
    "w": ("sbuf", [128, 520], "bfloat16"), "pc": ("sbuf", [128, 512], "float8_e4m3fn_x4"), "ps": ("sbuf", [128, 512], "uint8"),
    "zc": ("sbuf", [128, 512], "float32"), "dm": ("sbuf", [128, 512], "float32"),
    "ta": ("sbuf", [128, 512], "bfloat16"), "tb": ("sbuf", [128, 512], "bfloat16"),
    "sc": ("sbuf", [128, W + CA], "float8_e4m3fn_x4"), "ss": ("sbuf", [128, W + CA], "uint8"),
    "ac": ("sbuf", [128, 128], "float8_e4m3fn_x4"), "as": ("sbuf", [128, 128], "uint8"),
    "rc": ("sbuf", [128, 128], "float8_e4m3fn_x4"), "rs": ("sbuf", [128, 128], "uint8"),
    "yo": ("sbuf", [128, 512], "float32"),
    "pz": ("psum", [128, 2048], "float32"), "pd": ("psum", [128, 2048], "float32"),
}
SEMAPHORES = (["lv", "lq", "one", "sel", "zero", "qv", "qp", "qq", "adda", "addb", "qa", "qst", "arr", "sent", "sta", "stb"]
              + ["in%d" % i for i in range(3)]
              + [n + str(b) for n in ("lk", "qk", "z", "c", "d", "m", "n", "y", "e") for b in range(4)])


def plan(T, topo):
    hops = []
    for src, dst in zip(T.cores[:-1], T.cores[1:]):
        near = far = None
        e0 = 0
        if not topo.may_write(src, dst):
            own = [c for c in range(SIM_CORES) if topo.host(c) == topo.host(src) and topo.chip(c) == topo.chip(src)
                   and topo.may_write(c, dst)]
            near = [c for c in own if topo.die(c) == topo.die(src)][0]
            far = [c for c in own if topo.die(c) != topo.die(src)][0]
            e0 = NE
        hops.append((src, dst, [(True, "c", 0, CA, near, 0), (False, "c", CA, W, near, 0), (False, "s", 0, W, far, e0)]))
    return hops


def send(g, T, topo, core, to, out, in_, rsem, e0=0):
    bits = [b for b in range(16) if topo.mask(core, to) >> b & 1][e0:e0 + NE]
    rid, pid = topo.addr(to, core)
    g.remote_dma(out, in_, rsem, T.sem.sent, pid, rid, sum(1 << b for b in bits))


def view(T, kind, buf, lo, hi):
    return T[buf + "c"][:, lo:hi].bitcast(dt.uint8) if kind == "c" else T[buf + "s"][:, lo:hi]


def rank_program(g, core, T, topo):
    sem = T.sem
    hops = plan(T, topo)
    rank = T.rank_of(core)
    if rank is None:
        sent = 0
        for src, dst, pieces in hops:
            for i, (_, kind, lo, hi, via, _) in enumerate(pieces):
                if via == core:
                    g.wait_ge(sem["in%d" % i], NE)
                    send(g, T, topo, core, dst, view(T, kind, "a", lo, hi), view(T, kind, "r", lo, hi), sem.arr)
                    sent += NE
        if sent:
            g.wait_ge(sem.sent, sent)
        return

    te, ve, sc, sy = g.tensor, g.vector, g.scalar, g.sync
    copy = ActivationFunctionType.Copy
    last = rank == len(hops)

    def w(a, b=W):
        return slice(a * b, a * b + b)

    def part(a, lo, hi):
        return slice(a * W + lo, a * W + hi)

    def bank(buf, b, lo=0, hi=W):
        return buf[:, 512 * b + lo:512 * b + hi]

    sy.dma_start(T.vt[:], T.v[:]).then_inc(sem.lv, 16)
    for b in range(4):
        (sc if b % 2 == 0 else sy).dma_start(T.kt[:, w(b, 512)], T.k[:, w(b, 512)]).then_inc(sem["lk%d" % b], 16)
    if rank == 0:
        for b in range(4):
            sy.wait_ge(sem["lk%d" % b], 16)
    sy.dma_start(T.qt[:], T.q[:]).then_inc(sem.lq, 16)

    if rank > 0:
        ve.memset(T.w[:], 1.0).then_inc(sem.one, 1)
        g.wait_ge(sem.one, 1)
        g.affine_select(T.w[:], T.w[:], [[-1, 520]], AluOpType.is_equal, 0.0, 3, 4).then_inc(sem.sel, 1)
    if not last:
        ve.memset(T.ta[:, 4 * CA:512], 0.0).then_inc(sem.zero, 1)
        ve.memset(T.tb[:, 4 * (W - CA):512], 0.0).then_inc(sem.zero, 1)
    ve.wait_ge(sem.lv, 16)
    ve.quantize_mx(T.vc[:], T.vs[:], T.vt[:]).then_inc(sem.qv, 1)
    for b in range(4):
        ve.wait_ge(sem["lk%d" % b], 16)
        ve.quantize_mx(T.kc[:, w(b)], T.ks[:, w(b)], T.kt[:, w(b, 512)]).then_inc(sem["qk%d" % b], 1)
    if rank > 0:
        ve.wait_ge(sem.sel, 1)
        for b in range(4):
            ve.quantize_mx(T.pc[:, w(b)], T.ps[:, w(b)], T.w[:, 3 - b:3 - b + 512]).then_inc(sem.qp, 1)
        ve.wait_ge(sem.lq, 16)
        ve.quantize_mx(T.qc[:], T.qs[:], T.qt[:]).then_inc(sem.qq, 1)
    if not last:
        ve.wait_ge(sem.zero, 2)

    te.wait_ge(sem.qv, 1)
    for b in range(4):
        te.wait_ge(sem["qk%d" % b], 1)
        te.matmul_mx(bank(T.pz, b), T.kc[:, w(b)], T.ks[:, w(b)], T.vc[:], T.vs[:], True, True).then_inc(sem["z%d" % b], 1)

    def strip(b):
        return T.ta[:, b:4 * CA:4]

    def others(b):
        return T.tb[:, b:4 * (W - CA):4]

    def quantise_strip():
        ve.quantize_mx(T.sc[:, 0:W], T.ss[:, 0:W], T.ta[:]).then_inc(sem.qa, 1)

    def quantise_others():
        ve.wait_ge(sem.qa, 1)
        ve.quantize_mx(T.sc[:, CA:CA + W], T.ss[:, CA:CA + W], T.tb[:]).then_inc(sem.qst, 1)

    if rank == 0:
        for b in range(3):
            sc.wait_ge(sem["z%d" % b], 1)
            sc.activation(strip(b), bank(T.pz, b, 0, CA), copy, scale=0.023).then_inc(sem.adda, 1)
            sc.activation(others(b), bank(T.pz, b, CA, W), copy, scale=0.023).then_inc(sem["c%d" % b], 1)
        ve.wait_ge(sem.z3, 1)
        ve.tensor_scalar(strip(3), bank(T.pz, 3, 0, CA), 0.023, None, AluOpType.mult).then_inc(sem.adda, 1)
        ve.tensor_scalar(others(3), bank(T.pz, 3, CA, W), 0.023, None, AluOpType.mult).then_inc(sem.c3, 1)
        ve.wait_ge(sem.adda, 4)
        quantise_strip()
        for b in range(4):
            ve.wait_ge(sem["c%d" % b], 1)
        quantise_others()
    else:
        for b in range(4):
            sc.wait_ge(sem["z%d" % b], 1)
            sc.activation(T.zc[:, w(b)], bank(T.pz, b), copy, scale=0.023).then_inc(sem["c%d" % b], 1)
        te.wait_ge(sem.qp, 4)
        te.wait_ge(sem.arr, NE * len(hops[rank - 1][2]))
        for b in range(4):
            te.matmul_mx(bank(T.pd, b), T.pc[:, w(b)], T.ps[:, w(b)], T["ac"][:], T["as"][:], True, True).then_inc(sem["d%d" % b], 1)

        def scale(b, lo, hi, name):
            sc.activation(T.dm[:, part(b, lo, hi)], bank(T.pd, b, lo, hi), copy, scale=0.9).then_inc(sem["%s%d" % (name, b)], 1)

        for b in range(4):
            ve.wait_ge(sem["c%d" % b], 1)
        if last:
            for b in range(4):
                sc.wait_ge(sem["d%d" % b], 1)
                scale(b, 0, W, "m")
            for b in range(4):
                ve.wait_ge(sem["m%d" % b], 1)
                ve.tensor_tensor(T.ta[:, b:512:4], T.zc[:, w(b)], T.dm[:, w(b)], AluOpType.add).then_inc(sem.adda, 1)
            ve.wait_ge(sem.adda, 4)
            ve.quantize_mx(T.sc[:, 0:W], T.ss[:, 0:W], T.ta[:]).then_inc(sem.qst, 1)
        else:
            for b in range(4):
                sc.wait_ge(sem["d%d" % b], 1)
                scale(b, 0, W if b < 2 else CA, "m")
            for b in (2, 3):
                scale(b, CA, W, "n")
            for b in range(4):
                ve.wait_ge(sem["m%d" % b], 1)
                ve.tensor_tensor(strip(b), T.zc[:, part(b, 0, CA)], T.dm[:, part(b, 0, CA)], AluOpType.add).then_inc(sem.adda, 1)
            ve.wait_ge(sem.adda, 4)
            quantise_strip()
            for b in range(4):
                if b >= 2:
                    ve.wait_ge(sem["n%d" % b], 1)
                ve.tensor_tensor(others(b), T.zc[:, part(b, CA, W)], T.dm[:, part(b, CA, W)], AluOpType.add).then_inc(sem.addb, 1)
            ve.wait_ge(sem.addb, 4)
            quantise_others()

    if not last:
        _, dst, pieces = hops[rank]
        for i, (ahead, kind, lo, hi, via, e0) in enumerate(pieces):
            g.wait_ge(sem.qa if ahead else sem.qst, 1)
            if via is None:
                send(g, T, topo, core, dst, view(T, kind, "a", lo, hi), view(T, kind, "s", lo, hi), sem.arr)
            else:
                send(g, T, topo, core, via, view(T, kind, "r", lo, hi), view(T, kind, "s", lo, hi), sem["in%d" % i], e0)
        g.wait_ge(sem.sent, NE * len(pieces))

    if rank == 0:
        ve.wait_ge(sem.lq, 16)
        ve.quantize_mx(T.qc[:], T.qs[:], T.qt[:]).then_inc(sem.qq, 1)
    for b in range(4):
        te.wait_ge(sem["c%d" % b], 1)
    te.wait_ge(sem.qq, 1)
    if not last:
        te.wait_ge(sem.qa, 1)
    te.wait_ge(sem.qst, 1)
    for b in range(4):
        te.matmul_mx(bank(T.pz, b), T.sc[:, 0:W], T.ss[:, 0:W], T.qc[:, w(b)], T.qs[:, w(b)], True, True).then_inc(sem["y%d" % b], 1)
    for b in range(4):
        if b % 2 == 0:
            sc.wait_ge(sem["y%d" % b], 1)
            sc.activation(T.yo[:, w(b)], bank(T.pz, b), copy).then_inc(sem["e%d" % b], 1)
        else:
            ve.wait_ge(sem["y%d" % b], 1)
            ve.tensor_copy(T.yo[:, w(b)], bank(T.pz, b)).then_inc(sem["e%d" % b], 1)
    sy.wait_ge(sem.e0, 1)
    sy.wait_ge(sem.e1, 1)
    sy.dma_start(T.y[:, w(0, 256)], T.yo[:, w(0, 256)]).then_inc(sem.sta, 16)
    sc.wait_ge(sem.e2, 1)
    sc.wait_ge(sem.e3, 1)
    sc.dma_start(T.y[:, w(1, 256)], T.yo[:, w(1, 256)]).then_inc(sem.stb, 16)
    sy.wait_ge(sem.sta, 16)
    sc.wait_ge(sem.stb, 16)
